import numpy as np
import ml_dtypes


def mxq(x, axis, fmt="e4m3"):
    dtype, down = {"e4m3": (ml_dtypes.float8_e4m3fn, 7), "e5m2": (ml_dtypes.float8_e5m2, 14)}[fmt]
    v = np.moveaxis(np.asarray(x, np.float32).astype(ml_dtypes.bfloat16).astype(np.float64), axis, -1)
    blocks = v.reshape(v.shape[:-1] + (-1, 32))
    amax = np.abs(blocks).max(-1, keepdims=True)
    byte = np.maximum(np.where(amax > 0, np.frexp(amax)[1] - 1 + 127, 0) - down, 1)
    scale = np.exp2(byte - 127.0)
    codes = (blocks / scale).astype(np.float32).astype(dtype).astype(np.float64)
    return np.moveaxis((codes * scale).reshape(v.shape), -1, axis)


WIDE = False


def mx_kscale(k):
    if not WIDE:
        return np.ones(k)
    levels = np.array([10, -10, 5, -5, 0])
    if k % 512:
        return np.exp2(np.random.permutation(np.resize(levels, k // 32))).repeat(32)
    a = np.empty((k // 512, 16))
    for p in range(k // 512):
        a[p, :8] = np.random.permutation(np.resize(levels, 8))
        for g in range(8):
            far = levels[np.abs(levels - a[p, g]) >= 10]
            a[p, g + 8] = far[np.random.randint(len(far))]
    return np.exp2(a.ravel()).repeat(32)


def f64(x):
    return np.asarray(x).astype(np.float64)


def striped(idx):
    return np.tile(np.asarray(idx).reshape(-1, 16).T, (8, 1)).astype(np.uint16)


def unstriped(offs):
    return offs[:16].T.reshape(-1).astype(np.int64)


E2M1 = np.array([0.0, 0.5, 1.0, 1.5, 2.0, 3.0, 4.0, 6.0, -0.0, -0.5, -1.0, -1.5, -2.0, -3.0, -4.0, -6.0])


def pack_weight(w, fmt):
    k, n = w.shape
    w = f64(np.asarray(w, np.float32).astype(ml_dtypes.bfloat16)).reshape(k // 32, 32, n)
    amax = np.abs(w).max(1)
    if fmt == "e4m3":
        byte = np.frexp(amax)[1] - 1 + 127 - 7
    else:
        mant, ex = np.frexp(amax / 6.0)
        byte = np.where(mant > 0.5, ex, ex - 1) + 127
    byte = np.clip(np.where(amax > 0, byte, 1), 1, 254)
    scaled = (w * np.exp2(127.0 - byte)[:, None, :]).reshape(k, n).astype(np.float32)
    by_word = np.ascontiguousarray(scaled.reshape(k // 512, 128, 4, n).transpose(0, 1, 3, 2))
    if fmt == "e4m3":
        words = by_word.astype(ml_dtypes.float8_e4m3fn).view(np.uint8)
    else:
        c = by_word.astype(ml_dtypes.float4_e2m1fn).view(np.uint8) & 0xF
        words = (c[..., 0::2] | (c[..., 1::2] << 4)).reshape(k // 512, 128, 2 * n)
    return np.ascontiguousarray(words), np.ascontiguousarray(byte.astype(np.uint8).reshape(k // 512, 16, n))


def unpack_weight(words, scales, fmt):
    g, _, n = scales.shape
    words = np.ascontiguousarray(words).reshape(g, 128, n, -1)
    if fmt == "e4m3":
        vals = words.view(ml_dtypes.float8_e4m3fn).astype(np.float64)
    else:
        nib = np.empty((g, 128, n, 4), np.uint8)
        nib[..., 0::2] = words & 0xF
        nib[..., 1::2] = words >> 4
        vals = E2M1[nib]
    vals = vals * np.repeat(np.exp2(scales.astype(np.float64) - 127.0), 8, axis=1)[..., None]
    return vals.transpose(0, 1, 3, 2).reshape(g * 512, n)


def softplus(v):
    return np.log(1.0 + np.exp(v))


D, T, I, Q, E, K = 512, 2048, 512, 512, 512, 64


def setup_inputs():
    n = np.random.standard_normal
    idx = np.random.permutation(T)[:I]
    fd = mx_kscale(D)
    fi = mx_kscale(I)
    ti = np.ones(T)
    ti[idx] = fi
    keysp = pack_weight(n((D, T)) / fd[:, None], "e4m3")
    return {
        "query": (n((D, Q)) * 1.0 / np.sqrt(D) * fd[:, None]).astype(np.float32),
        "keys_words": keysp[0],
        "keys_scales": keysp[1],
        "ceil_t": np.tile(np.random.uniform(1.0, 4.0, T), (128, 1)).astype(np.float32),
        "halfp": np.tile(np.random.uniform(0.4, 1.5, T), (128, 1)).astype(np.float32),
        "width": (np.random.uniform(0.3, 0.8, (Q, 1))).astype(np.float32),
        "os": (np.random.uniform(4.0, 16.0, (1, I)) * fi).astype(np.float32),
        "vals": (n((E, T)) / ti).astype(np.float32),
        "caution": (np.random.uniform(0.2, 0.8, (1, K))).astype(np.float32),
        "offs": striped(idx),
    }


def reference(query, keys_words, keys_scales, ceil_t, halfp, width, os, vals, caution, offs):
    idx = unstriped(offs)
    keysu = unpack_weight(keys_words, keys_scales, "e4m3")
    queryq = mxq(f64(query), 0, "e4m3")
    keysidxg = keysu[:, idx]
    a = queryq.T @ keysidxg
    fa = softplus(a * 2.0)
    s = fa * f64(ceil_t)[:1][:, idx] / (fa + f64(halfp)[:1][:, idx])
    ce = (s - np.mean(s, axis=1, keepdims=True)) / f64(width)
    p = 1.0 / (np.square(ce) + 1.0)
    w = p / np.sum(p, axis=1, keepdims=True)
    wo1 = w * f64(os)
    wt1 = wo1.T
    vt1 = f64(vals)[:, idx].T
    vt1q = mxq(vt1, 0, "e4m3")
    wt1q = mxq(wt1, 0, "e4m3")
    o = vt1q.T @ wt1q
    y = o.reshape(E, K, Q // K).max(axis=2) - o.reshape(E, K, Q // K).mean(axis=2) * f64(caution)
    return y

@@ -1,0 +1,265 @@
+from contextlib import ExitStack
+
+import concourse.mybir as mybir
+from concourse.masks import make_identity
+
+D, T, I, Q, E, K = 512, 2048, 512, 512, 512, 64
+FLOPS = 2 * Q * I * D + 2 * E * Q * I
+BYTES = 4 * (D * Q + 128 * T + E * T + 2 * T + Q + I + K + E * K) + 16 * T + 2 * 128 * 32
+
+F32 = mybir.dt.float32
+BF16 = mybir.dt.bfloat16
+I32 = mybir.dt.int32
+U32 = mybir.dt.uint32
+U16 = mybir.dt.uint16
+U8 = mybir.dt.uint8
+FP8X4 = mybir.dt.float8_e4m3fn_x4
+ACT = mybir.ActivationFunctionType
+ALU = mybir.AluOpType
+AX = mybir.AxisListType
+
+P = 128
+GROUP = Q // K
+HALF = Q // 2
+TINY = 2.0 ** -60
+
+
+def tile_attend_saturating_typical_groupbestread_kernel(
+    tc, query, keys_words, keys_scales, ceil_t, halfp, width, os_row, vals, caution, offs, out
+):
+    nc = tc.nc
+    with ExitStack() as ctx:
+        sb = ctx.enter_context(tc.tile_pool(name="sb", bufs=1))
+        ps = ctx.enter_context(tc.psum_pool(name="ps", bufs=1))
+
+        def tile(name, shape, dtype=F32, tag=None):
+            return sb.tile(shape, dtype, name=name, tag=tag or name, align_bytes=64)
+
+        def bank(tag, name, shape):
+            return ps.tile(shape, F32, name=name, tag=tag)
+
+        def add_transposed(dst, src, start, stop):
+            nc.tensor.matmul(dst, lhsT=src, rhs=ident[:], is_transpose=True, start=start, stop=stop)
+
+        offsets = tile("offsets", [P, I // 16], U16)
+        nc.sync.dma_start(offsets[:], offs)
+
+        key_scale_pool = tile("key_scale_pool", [P, T], U8)
+        nc.vector.memset(key_scale_pool[:].bitcast(I32), 0)
+        half_pool = tile("half_pool", [P, T])
+        ceil_pool = tile("ceil_pool", [P, T])
+        nc.gpsimd.memset(half_pool[0 : P - 1, :], 0.0)
+        nc.vector.memset(ceil_pool[0 : P - 1, :], 0.0)
+        tiny = tile("tiny", [P, 1])
+        nc.vector.memset(tiny[:], TINY)
+        ident = tile("ident", [P, P])
+        make_identity(nc, ident[:])
+
+        nc.sync.dma_start(half_pool[P - 1 : P, :], halfp[0:1, :])
+        nc.sync.dma_start(ceil_pool[P - 1 : P, :], ceil_t[0:1, :])
+        for quad in range(4):
+            nc.sync.dma_start(
+                key_scale_pool[32 * quad : 32 * quad + 4, :].bitcast(I32),
+                keys_scales[0, 4 * quad : 4 * quad + 4, :].bitcast(I32),
+            )
+        q_rows = query.rearrange("(p j) q -> p j q", j=4)
+        q_raw = tile("q_raw", [P, 4, Q])
+        key_pool = tile("key_pool", [P, T], I32)
+        nc.sync.dma_start(q_raw[:], q_rows)
+        nc.sync.dma_start(key_pool[:], keys_words[0].rearrange("p n t -> p (n t)").bitcast(I32))
+        width_cols = tile("width_cols", [P, 4])
+        nc.sync.dma_start(
+            width_cols[:], width.rearrange("(j p) o -> p (j o)", p=P), allow_slow_non_contiguous=True
+        )
+        val_rows = vals.rearrange("(p j) t -> j p t", j=4)
+        val_pool = [tile(f"val_pool{b}", [P, T]) for b in range(4)]
+        for b in range(4):
+            nc.sync.dma_start(val_pool[b][:], val_rows[b])
+        os_rows = tile("os_rows", [P, I])
+        nc.sync.dma_start(os_rows[:], os_row[0].partition_broadcast(P))
+        caution_rows = tile("caution_rows", [P, K])
+        nc.sync.dma_start(caution_rows[:], caution[0].partition_broadcast(P))
+
+        cols_of = {}
+        for name, pool, tag in (("half", half_pool, "side0"), ("ceil", ceil_pool, "side1")):
+            picked = tile(f"{name}_picked", [P, I])
+            nc.scalar.activation(picked[:], pool[:].indirect(offsets[:]), ACT.Copy)
+            turned = bank(tag, f"{name}_turned", [P, 4, P])
+            for s in range(4):
+                nc.tensor.transpose(turned[:, s, :], picked[:, s * P : (s + 1) * P], ident[:])
+            cols_of[name] = turned[:, :, P - 1]
+        neg_half = tile("neg_half", [P, 4])
+        nc.scalar.activation(neg_half[:], cols_of["half"], ACT.Copy, scale=-1.0)
+        ceil_cols = tile("ceil_cols", [P, 4])
+        ceil_sum = tile("ceil_sum", [P, 1])
+        nc.scalar.activation(ceil_cols[:], cols_of["ceil"], ACT.Identity, accum_out=ceil_sum[:])
+        neg_ch = tile("neg_ch", [P, 4])
+        nc.gpsimd.tensor_tensor(neg_ch[:], neg_half[:], ceil_cols[:], ALU.mult)
+
+        key_scales = tile("key_scales", [P, I], U8)
+        nc.vector.tensor_copy(key_scales[:], key_scale_pool[:].indirect(offsets[:]))
+
+        q_codes = tile("q_codes", [P, Q], U32)
+        q_scales = tile("q_scales", [P, Q], U8)
+        for h in range(2):
+            q_bf = tile(f"q_bf{h}", [P, HALF, 4], BF16)
+            cols = slice(h * HALF, (h + 1) * HALF)
+            nc.vector.tensor_copy(
+                q_bf[:].rearrange("p (c i) t -> p c t i", i=4),
+                q_raw[:, :, cols].rearrange("p t (c i) -> p c t i", i=4),
+            )
+            nc.vector.quantize_mx(
+                out=q_codes[:, cols].bitcast(FP8X4),
+                scales=q_scales[:, cols],
+                in_=q_bf[:].rearrange("p c t -> p (c t)"),
+            )
+
+        key_codes = tile("key_codes", [P, I], U32)
+        sig = [tile(f"sig{g}", [P, 2, Q]) for g in range(2)]
+        score = []
+        for s in range(4):
+            cols = slice(s * P, (s + 1) * P)
+            nc.vector.tensor_copy(
+                key_codes[:, cols], key_pool[:].bitcast(U32).indirect(offsets[:, 8 * s : 8 * (s + 1)])
+            )
+            score.append(bank(f"main{s}", f"score{s}", [P, Q]))
+            nc.tensor.matmul_mx(
+                score[s][:],
+                lhsT=key_codes[:, cols].bitcast(FP8X4),
+                lhsT_scale=key_scales[:, cols],
+                rhs=q_codes[:].bitcast(FP8X4),
+                rhs_scale=q_scales[:],
+                start=True,
+                stop=True,
+            )
+            nc.scalar.activation(sig[s % 2][:, s // 2, :], score[s][:], ACT.Sigmoid, scale=-2.0)
+
+        v_codes = tile("v_codes", [P, E], U32)
+        v_scales = tile("v_scales", [P, E], U8)
+
+        def quantise_values(b, tag, gather_on_scalar, copy_on_scalar):
+            v_picked = tile(f"v_picked{b}", [P, I], BF16, tag=tag)
+            if gather_on_scalar:
+                nc.scalar.activation(v_picked[:], val_pool[b][:].indirect(offsets[:]), ACT.Copy)
+            else:
+                nc.vector.tensor_copy(v_picked[:], val_pool[b][:].indirect(offsets[:]))
+            v_turned = bank(f"turn{b % 2}", f"v_turned{b}", [P, 2, P])
+            for u in range(2):
+                nc.tensor.transpose(v_turned[:, u, :], v_picked[:].bitcast(F32)[:, u::2], ident[:])
+            v_bf = tile(f"v_bf{b}", [P, 4 * P], BF16)
+            copy = nc.scalar.copy if copy_on_scalar else nc.vector.tensor_copy
+            copy(v_bf[:].bitcast(F32).rearrange("p (e u) -> p e u", u=2), v_turned[:].rearrange("p u e -> p e u"))
+            cols = slice(b * P, (b + 1) * P)
+            nc.vector.quantize_mx(out=v_codes[:, cols].bitcast(FP8X4), scales=v_scales[:, cols], in_=v_bf[:])
+
+        quantise_values(0, None, False, False)
+        quantise_values(1, None, False, False)
+
+        neg_fa = {}
+        for g in range(2):
+            log_sig = tile(f"log_sig{g}", [P, 2, Q])
+            nc.scalar.activation(log_sig[:], sig[g][:], ACT.Ln, bias=tiny[:])
+            for r in range(2):
+                s = 2 * r + g
+                neg_fa[s] = tile(f"neg_fa{s}", [P, Q])
+                nc.vector.scalar_tensor_tensor(neg_fa[s][:], score[s][:], -2.0, log_sig[:, r, :], ALU.mult, ALU.min)
+
+        inv_width = tile("inv_width", [P, 4])
+        nc.vector.reciprocal(inv_width[:], width_cols[:])
+
+        s_bank, row_sum = {}, {}
+        for h in range(2):
+            row_sum[h] = bank(f"side{h}", f"row_sum{h}", [P, 2, P])
+            for jj in range(2):
+                j = 2 * h + jj
+                s_bank[j] = bank(f"main{j}", f"s_bank{j}", [P, 4, P])
+                for s in range(4):
+                    add_transposed(s_bank[j][:, s, :], ceil_cols[:, s : s + 1].to_broadcast([P, P]), s == 0, False)
+                add_transposed(row_sum[h][:, jj, :], ceil_sum[:].to_broadcast([P, P]), jj == 0, False)
+            for s in range(4):
+                root = tile(f"root{h}{s}", [P, HALF])
+                nc.scalar.activation(
+                    root[:],
+                    neg_fa[s][:, h * HALF : (h + 1) * HALF],
+                    ACT.Abs_reciprocal_sqrt,
+                    bias=neg_half[:, s : s + 1],
+                )
+                drop = tile(f"drop{h}{s}", [P, HALF])
+                nc.vector.scalar_tensor_tensor(drop[:], root[:], neg_ch[:, s : s + 1], root[:], ALU.mult, ALU.mult)
+                for jj in range(2):
+                    add_transposed(row_sum[h][:, jj, :], drop[:, jj * P : (jj + 1) * P], False, s == 3 and jj == 1)
+                for jj in range(2):
+                    add_transposed(s_bank[2 * h + jj][:, s, :], drop[:, jj * P : (jj + 1) * P], False, s == 3)
+
+        shifts = []
+        for h in range(2):
+            total = tile(f"total{h}", [P, 2])
+            nc.vector.tensor_reduce(total[:], row_sum[h][:], AX.X, ALU.add)
+            shifts.append(tile(f"shift{h}", [P, 2]))
+            nc.vector.scalar_tensor_tensor(
+                shifts[h][:], total[:], -1.0 / I, inv_width[:, 2 * h : 2 * h + 2], ALU.mult, ALU.mult
+            )
+        quantise_values(2, "root12", False, True)
+        quantise_values(3, "root13", False, True)
+
+        result = tile("result", [P, 4, K])
+        for h in range(2):
+            shift = shifts[h]
+            for jj in range(2):
+                j = 2 * h + jj
+                z_sq = tile(f"z_sq{j}", [P, I])
+                nc.scalar.activation(
+                    z_sq[:],
+                    s_bank[j][:].rearrange("p s i -> p (s i)"),
+                    ACT.Square,
+                    bias=shift[:, jj : jj + 1],
+                    scale=inv_width[:, j : j + 1],
+                )
+                part_root = tile(f"part_root{j}", [P, I])
+                nc.scalar.activation(part_root[:], z_sq[:], ACT.Abs_reciprocal_sqrt, bias=1.0)
+                part = tile(f"part{j}", [P, I])
+                part_sum = tile(f"part_sum{j}", [P, 1])
+                nc.scalar.activation(part[:], part_root[:], ACT.Square, accum_out=part_sum[:])
+                inv_sum = tile(f"inv_sum{j}", [P, 1])
+                nc.vector.reciprocal(inv_sum[:], part_sum[:])
+                w_rows = tile(f"w_rows{j}", [P, I], BF16)
+                nc.vector.scalar_tensor_tensor(w_rows[:], part[:], inv_sum[:], os_rows[:], ALU.mult, ALU.mult)
+                w_turned = bank(f"turn{j % 2}", f"w_turned{j}", [P, 2, P])
+                for u in range(2):
+                    nc.tensor.transpose(w_turned[:, u, :], w_rows[:].bitcast(F32)[:, u::2], ident[:])
+                w_bf = tile(f"w_bf{j}", [P, 4 * P], BF16)
+                nc.scalar.copy(
+                    w_bf[:].bitcast(F32).rearrange("p (q u) -> p q u", u=2), w_turned[:].rearrange("p u q -> p q u")
+                )
+                w_codes = tile(f"w_codes{j}", [P, P], U32)
+                w_scales = tile(f"w_scales{j}", [P, P], U8)
+                nc.vector.quantize_mx(out=w_codes[:].bitcast(FP8X4), scales=w_scales[:], in_=w_bf[:])
+                o_bank = bank(f"main{j}", f"o_bank{j}", [P, 4, P])
+                for b in range(4):
+                    cols = slice(b * P, (b + 1) * P)
+                    nc.tensor.matmul_mx(
+                        o_bank[:, b, :],
+                        lhsT=v_codes[:, cols].bitcast(FP8X4),
+                        lhsT_scale=v_scales[:, cols],
+                        rhs=w_codes[:].bitcast(FP8X4),
+                        rhs_scale=w_scales[:],
+                        start=True,
+                        stop=True,
+                    )
+                groups = o_bank[:].rearrange("p b (k g) -> p b k g", g=GROUP)
+                ks = slice(16 * j, 16 * (j + 1))
+                best = tile(f"best{j}", [P, 4, 16])
+                nc.vector.tensor_reduce(best[:], groups, AX.X, ALU.max)
+                sums = tile(f"sums{j}", [P, 4, 16])
+                nc.vector.tensor_reduce(sums[:], groups, AX.X, ALU.add)
+                penalty = tile(f"penalty{j}", [P, 4, 16])
+                nc.vector.scalar_tensor_tensor(
+                    penalty[:],
+                    sums[:],
+                    -1.0 / GROUP,
+                    caution_rows[:, ks].unsqueeze(1).to_broadcast([P, 4, 16]),
+                    ALU.mult,
+                    ALU.mult,
+                )
+                nc.vector.tensor_tensor(result[:, :, ks], best[:], penalty[:], ALU.add)
+        nc.sync.dma_start(out.rearrange("(p j) k -> p j k", j=4), result[:])

@@ -45,10 +45,10 @@ def tile_attend_saturating_typical_groupbestread_kernel(
         nc.sync.dma_start(offsets[:], offs)
 
         key_scale_pool = tile("key_scale_pool", [P, T], U8)
-        nc.vector.memset(key_scale_pool[:].bitcast(I32), 0)
+        nc.gpsimd.memset(key_scale_pool[:].bitcast(I32), 0)
         half_pool = tile("half_pool", [P, T])
         ceil_pool = tile("ceil_pool", [P, T])
-        nc.gpsimd.memset(half_pool[0 : P - 1, :], 0.0)
+        nc.vector.memset(half_pool[0 : P - 1, :], 0.0)
         nc.vector.memset(ceil_pool[0 : P - 1, :], 0.0)
         tiny = tile("tiny", [P, 1])
         nc.vector.memset(tiny[:], TINY)
@@ -63,10 +63,11 @@ def tile_attend_saturating_typical_groupbestread_kernel(
                 keys_scales[0, 4 * quad : 4 * quad + 4, :].bitcast(I32),
             )
         q_rows = query.rearrange("(p j) q -> p j q", j=4)
-        q_raw = tile("q_raw", [P, 4, Q])
+        q_raw = [tile(f"q_raw{h}", [P, 4, HALF]) for h in range(2)]
         key_pool = tile("key_pool", [P, T], I32)
-        nc.sync.dma_start(q_raw[:], q_rows)
+        nc.sync.dma_start(q_raw[0][:], q_rows[:, :, 0:HALF])
         nc.sync.dma_start(key_pool[:], keys_words[0].rearrange("p n t -> p (n t)").bitcast(I32))
+        nc.sync.dma_start(q_raw[1][:], q_rows[:, :, HALF:Q])
         width_cols = tile("width_cols", [P, 4])
         nc.sync.dma_start(
             width_cols[:], width.rearrange("(j p) o -> p (j o)", p=P), allow_slow_non_contiguous=True
@@ -88,178 +89,235 @@ def tile_attend_saturating_typical_groupbestread_kernel(
             for s in range(4):
                 nc.tensor.transpose(turned[:, s, :], picked[:, s * P : (s + 1) * P], ident[:])
             cols_of[name] = turned[:, :, P - 1]
-        neg_half = tile("neg_half", [P, 4])
+
+        key_scales = tile("key_scales", [P, I], U8)
+        nc.vector.tensor_copy(key_scales[:], key_scale_pool[:].indirect(offsets[:]))
+
+        key_codes = tile("key_codes", [P, I], U32)
+        sig = [tile(f"sig{g}", [P, 2, 2 * HALF]) for g in range(2)]
+        score = {}
+        for h in range(2):
+            q_bf = tile(f"q_bf{h}", [P, HALF, 4], BF16)
+            nc.vector.tensor_copy(
+                q_bf[:].rearrange("p (c i) t -> p c t i", i=4),
+                q_raw[h][:].rearrange("p t (c i) -> p c t i", i=4),
+            )
+            q_codes = tile(f"q_codes{h}", [P, HALF], U32)
+            q_scales = tile(f"q_scales{h}", [P, HALF], U8)
+            nc.vector.quantize_mx(
+                out=q_codes[:].bitcast(FP8X4), scales=q_scales[:], in_=q_bf[:].rearrange("p c t -> p (c t)")
+            )
+            for g in range(2):
+                if h == 0:
+                    nc.vector.tensor_copy(
+                        key_codes[:, g * 256 : (g + 1) * 256],
+                        key_pool[:].bitcast(U32).indirect(offsets[:, 16 * g : 16 * (g + 1)]),
+                    )
+                score[h, g] = bank(f"main{2 * h + g}", f"score{h}{g}", [P, 2, HALF])
+                for r in range(2):
+                    cols = slice((2 * g + r) * P, (2 * g + r + 1) * P)
+                    nc.tensor.matmul_mx(
+                        score[h, g][:, r, :],
+                        lhsT=key_codes[:, cols].bitcast(FP8X4),
+                        lhsT_scale=key_scales[:, cols],
+                        rhs=q_codes[:].bitcast(FP8X4),
+                        rhs_scale=q_scales[:],
+                        start=True,
+                        stop=True,
+                    )
+                nc.scalar.activation(
+                    sig[g][:, h, :], score[h, g][:].rearrange("p r q -> p (r q)"), ACT.Sigmoid, scale=-2.0
+                )
+
+        neg_half = tile("neg_half", [P, 4], tag="q_scales1")
         nc.scalar.activation(neg_half[:], cols_of["half"], ACT.Copy, scale=-1.0)
-        ceil_cols = tile("ceil_cols", [P, 4])
+        ceil_cols = tile("ceil_cols", [P, 4], tag="q_codes1")
         ceil_sum = tile("ceil_sum", [P, 1])
         nc.scalar.activation(ceil_cols[:], cols_of["ceil"], ACT.Identity, accum_out=ceil_sum[:])
         neg_ch = tile("neg_ch", [P, 4])
         nc.gpsimd.tensor_tensor(neg_ch[:], neg_half[:], ceil_cols[:], ALU.mult)
 
-        key_scales = tile("key_scales", [P, I], U8)
-        nc.vector.tensor_copy(key_scales[:], key_scale_pool[:].indirect(offsets[:]))
-
-        q_codes = tile("q_codes", [P, Q], U32)
-        q_scales = tile("q_scales", [P, Q], U8)
-        for h in range(2):
-            q_bf = tile(f"q_bf{h}", [P, HALF, 4], BF16)
-            cols = slice(h * HALF, (h + 1) * HALF)
-            nc.vector.tensor_copy(
-                q_bf[:].rearrange("p (c i) t -> p c t i", i=4),
-                q_raw[:, :, cols].rearrange("p t (c i) -> p c t i", i=4),
-            )
-            nc.vector.quantize_mx(
-                out=q_codes[:, cols].bitcast(FP8X4),
-                scales=q_scales[:, cols],
-                in_=q_bf[:].rearrange("p c t -> p (c t)"),
-            )
-
-        key_codes = tile("key_codes", [P, I], U32)
-        sig = [tile(f"sig{g}", [P, 2, Q]) for g in range(2)]
-        score = []
-        for s in range(4):
-            cols = slice(s * P, (s + 1) * P)
-            nc.vector.tensor_copy(
-                key_codes[:, cols], key_pool[:].bitcast(U32).indirect(offsets[:, 8 * s : 8 * (s + 1)])
-            )
-            score.append(bank(f"main{s}", f"score{s}", [P, Q]))
-            nc.tensor.matmul_mx(
-                score[s][:],
-                lhsT=key_codes[:, cols].bitcast(FP8X4),
-                lhsT_scale=key_scales[:, cols],
-                rhs=q_codes[:].bitcast(FP8X4),
-                rhs_scale=q_scales[:],
-                start=True,
-                stop=True,
-            )
-            nc.scalar.activation(sig[s % 2][:, s // 2, :], score[s][:], ACT.Sigmoid, scale=-2.0)
-
         v_codes = tile("v_codes", [P, E], U32)
         v_scales = tile("v_scales", [P, E], U8)
 
-        def quantise_values(b, tag, gather_on_scalar, copy_on_scalar):
+        v_turned = {}
+
+        def turn_values(b, tag=None):
             v_picked = tile(f"v_picked{b}", [P, I], BF16, tag=tag)
-            if gather_on_scalar:
-                nc.scalar.activation(v_picked[:], val_pool[b][:].indirect(offsets[:]), ACT.Copy)
-            else:
-                nc.vector.tensor_copy(v_picked[:], val_pool[b][:].indirect(offsets[:]))
-            v_turned = bank(f"turn{b % 2}", f"v_turned{b}", [P, 2, P])
+            nc.vector.tensor_copy(v_picked[:], val_pool[b][:].indirect(offsets[:]))
+            if b < 3:
+                v_turned[b] = bank(f"turn{b % 2}", f"v_turned{b}", [P, 2, 2, P])
             for u in range(2):
-                nc.tensor.transpose(v_turned[:, u, :], v_picked[:].bitcast(F32)[:, u::2], ident[:])
-            v_bf = tile(f"v_bf{b}", [P, 4 * P], BF16)
-            copy = nc.scalar.copy if copy_on_scalar else nc.vector.tensor_copy
-            copy(v_bf[:].bitcast(F32).rearrange("p (e u) -> p e u", u=2), v_turned[:].rearrange("p u e -> p e u"))
-            cols = slice(b * P, (b + 1) * P)
+                nc.tensor.transpose(v_turned[min(b, 2)][:, b // 3, u, :], v_picked[:].bitcast(F32)[:, u::2], ident[:])
+
+        def quantise_values(first, n, copy, tag=None):
+            v_bf = tile(f"v_bf{first}", [P, n * 4 * P], BF16, tag=tag)
+            copy(
+                v_bf[:].bitcast(F32).rearrange("p (b e u) -> p b e u", b=n, u=2),
+                v_turned[first][:, 0:n].rearrange("p b u e -> p b e u"),
+            )
+            cols = slice(first * P, (first + n) * P)
             nc.vector.quantize_mx(out=v_codes[:, cols].bitcast(FP8X4), scales=v_scales[:, cols], in_=v_bf[:])
 
-        quantise_values(0, None, False, False)
-        quantise_values(1, None, False, False)
+        turn_values(0)
+        quantise_values(0, 1, nc.vector.tensor_copy)
+        turn_values(1)
+
+        s_tags = ["side0", "side1", "main0", "main2"]
+        s_bank = {}
+
+        def open_s_bank(j):
+            s_bank[j] = bank(s_tags[j], f"s_bank{j}", [P, 4, P])
+            for s in range(4):
+                add_transposed(s_bank[j][:, s, :], ceil_cols[:, s : s + 1].to_broadcast([P, P]), s == 0, False)
+
+        open_s_bank(0)
+        open_s_bank(1)
 
         neg_fa = {}
         for g in range(2):
             log_sig = tile(f"log_sig{g}", [P, 2, Q])
             nc.scalar.activation(log_sig[:], sig[g][:], ACT.Ln, bias=tiny[:])
-            for r in range(2):
-                s = 2 * r + g
-                neg_fa[s] = tile(f"neg_fa{s}", [P, Q])
-                nc.vector.scalar_tensor_tensor(neg_fa[s][:], score[s][:], -2.0, log_sig[:, r, :], ALU.mult, ALU.min)
+            for h in range(2):
+                neg_fa[h, g] = tile(f"neg_fa{h}{g}", [P, 2, HALF])
+                nc.vector.scalar_tensor_tensor(
+                    neg_fa[h, g][:].rearrange("p r q -> p (r q)"),
+                    score[h, g][:].rearrange("p r q -> p (r q)"),
+                    -2.0,
+                    log_sig[:, h, :],
+                    ALU.mult,
+                    ALU.min,
+                )
 
+        quantise_values(1, 1, nc.vector.tensor_copy, "log_sig1")
         inv_width = tile("inv_width", [P, 4])
         nc.vector.reciprocal(inv_width[:], width_cols[:])
 
-        s_bank, row_sum = {}, {}
-        for h in range(2):
-            row_sum[h] = bank(f"side{h}", f"row_sum{h}", [P, 2, P])
-            for jj in range(2):
-                j = 2 * h + jj
-                s_bank[j] = bank(f"main{j}", f"s_bank{j}", [P, 4, P])
-                for s in range(4):
-                    add_transposed(s_bank[j][:, s, :], ceil_cols[:, s : s + 1].to_broadcast([P, P]), s == 0, False)
-                add_transposed(row_sum[h][:, jj, :], ceil_sum[:].to_broadcast([P, P]), jj == 0, False)
+        shifts = {}
+        for c, (tiles, sum_tag) in enumerate((((0,), None), ((1,), None), ((2, 3), None))):
+            n = len(tiles)
+            if sum_tag:
+                row_sum = bank(sum_tag, f"row_sum{c}", [P, n, P])
+            for jj, j in enumerate(tiles):
+                if j not in s_bank:
+                    open_s_bank(j)
+                if sum_tag:
+                    add_transposed(row_sum[:, jj, :], ceil_sum[:].to_broadcast([P, P]), jj == 0, False)
             for s in range(4):
-                root = tile(f"root{h}{s}", [P, HALF])
+                root = tile(f"root{c}{s}", [P, n * P])
                 nc.scalar.activation(
                     root[:],
-                    neg_fa[s][:, h * HALF : (h + 1) * HALF],
+                    neg_fa[tiles[0] // 2, s // 2][:, s % 2, tiles[0] % 2 * P : (tiles[0] % 2 + n) * P],
                     ACT.Abs_reciprocal_sqrt,
                     bias=neg_half[:, s : s + 1],
                 )
-                drop = tile(f"drop{h}{s}", [P, HALF])
+                drop = tile(f"drop{c}{s}", [P, n * P])
                 nc.vector.scalar_tensor_tensor(drop[:], root[:], neg_ch[:, s : s + 1], root[:], ALU.mult, ALU.mult)
-                for jj in range(2):
-                    add_transposed(row_sum[h][:, jj, :], drop[:, jj * P : (jj + 1) * P], False, s == 3 and jj == 1)
-                for jj in range(2):
-                    add_transposed(s_bank[2 * h + jj][:, s, :], drop[:, jj * P : (jj + 1) * P], False, s == 3)
-
-        shifts = []
-        for h in range(2):
-            total = tile(f"total{h}", [P, 2])
-            nc.vector.tensor_reduce(total[:], row_sum[h][:], AX.X, ALU.add)
-            shifts.append(tile(f"shift{h}", [P, 2]))
-            nc.vector.scalar_tensor_tensor(
-                shifts[h][:], total[:], -1.0 / I, inv_width[:, 2 * h : 2 * h + 2], ALU.mult, ALU.mult
-            )
-        quantise_values(2, "root12", False, True)
-        quantise_values(3, "root13", False, True)
+                for jj in range(n if sum_tag else 0):
+                    add_transposed(row_sum[:, jj, :], drop[:, jj * P : (jj + 1) * P], False, s == 3 and jj == n - 1)
+                for jj, j in enumerate(tiles):
+                    add_transposed(s_bank[j][:, s, :], drop[:, jj * P : (jj + 1) * P], False, s == 3)
+            if sum_tag:
+                total = tile(f"total{c}", [P, n])
+                nc.vector.tensor_reduce(total[:], row_sum[:], AX.X, ALU.add)
+                shift = tile(f"shift{c}", [P, n])
+                nc.vector.scalar_tensor_tensor(
+                    shift[:], total[:], -1.0 / I, inv_width[:, tiles[0] : tiles[0] + n], ALU.mult, ALU.mult
+                )
+                for jj, j in enumerate(tiles):
+                    shifts[j] = shift[:, jj : jj + 1]
+            else:
+                for j in tiles:
+                    total = tile(f"total{j}", [P, 1])
+                    nc.vector.tensor_reduce(total[:], s_bank[j][:].rearrange("p s i -> p (s i)"), AX.X, ALU.add)
+                    shift = tile(f"shift{j}", [P, 1])
+                    nc.vector.scalar_tensor_tensor(shift[:], total[:], -1.0 / I, inv_width[:, j : j + 1], ALU.mult, ALU.mult)
+                    shifts[j] = shift[:]
+        turn_values(2, "total0")
+        turn_values(3, "total1")
+        quantise_values(2, 2, nc.scalar.copy, None)
 
         result = tile("result", [P, 4, K])
-        for h in range(2):
-            shift = shifts[h]
-            for jj in range(2):
-                j = 2 * h + jj
-                z_sq = tile(f"z_sq{j}", [P, I])
-                nc.scalar.activation(
-                    z_sq[:],
-                    s_bank[j][:].rearrange("p s i -> p (s i)"),
-                    ACT.Square,
-                    bias=shift[:, jj : jj + 1],
-                    scale=inv_width[:, j : j + 1],
-                )
-                part_root = tile(f"part_root{j}", [P, I])
-                nc.scalar.activation(part_root[:], z_sq[:], ACT.Abs_reciprocal_sqrt, bias=1.0)
-                part = tile(f"part{j}", [P, I])
-                part_sum = tile(f"part_sum{j}", [P, 1])
-                nc.scalar.activation(part[:], part_root[:], ACT.Square, accum_out=part_sum[:])
-                inv_sum = tile(f"inv_sum{j}", [P, 1])
-                nc.vector.reciprocal(inv_sum[:], part_sum[:])
-                w_rows = tile(f"w_rows{j}", [P, I], BF16)
-                nc.vector.scalar_tensor_tensor(w_rows[:], part[:], inv_sum[:], os_rows[:], ALU.mult, ALU.mult)
-                w_turned = bank(f"turn{j % 2}", f"w_turned{j}", [P, 2, P])
-                for u in range(2):
-                    nc.tensor.transpose(w_turned[:, u, :], w_rows[:].bitcast(F32)[:, u::2], ident[:])
-                w_bf = tile(f"w_bf{j}", [P, 4 * P], BF16)
-                nc.scalar.copy(
-                    w_bf[:].bitcast(F32).rearrange("p (q u) -> p q u", u=2), w_turned[:].rearrange("p u q -> p q u")
-                )
-                w_codes = tile(f"w_codes{j}", [P, P], U32)
-                w_scales = tile(f"w_scales{j}", [P, P], U8)
-                nc.vector.quantize_mx(out=w_codes[:].bitcast(FP8X4), scales=w_scales[:], in_=w_bf[:])
-                o_bank = bank(f"main{j}", f"o_bank{j}", [P, 4, P])
-                for b in range(4):
-                    cols = slice(b * P, (b + 1) * P)
-                    nc.tensor.matmul_mx(
-                        o_bank[:, b, :],
-                        lhsT=v_codes[:, cols].bitcast(FP8X4),
-                        lhsT_scale=v_scales[:, cols],
-                        rhs=w_codes[:].bitcast(FP8X4),
-                        rhs_scale=w_scales[:],
-                        start=True,
-                        stop=True,
-                    )
-                groups = o_bank[:].rearrange("p b (k g) -> p b k g", g=GROUP)
-                ks = slice(16 * j, 16 * (j + 1))
-                best = tile(f"best{j}", [P, 4, 16])
-                nc.vector.tensor_reduce(best[:], groups, AX.X, ALU.max)
-                sums = tile(f"sums{j}", [P, 4, 16])
-                nc.vector.tensor_reduce(sums[:], groups, AX.X, ALU.add)
-                penalty = tile(f"penalty{j}", [P, 4, 16])
+        held = {}
+
+        def parts(j):
+            z_sq = tile(f"z_sq{j}", [P, I])
+            nc.scalar.activation(
+                z_sq[:],
+                s_bank[j][:].rearrange("p s i -> p (s i)"),
+                ACT.Square,
+                bias=shifts[j],
+                scale=inv_width[:, j : j + 1],
+            )
+            part_root = tile(f"part_root{j}", [P, I])
+            nc.scalar.activation(part_root[:], z_sq[:], ACT.Abs_reciprocal_sqrt, bias=1.0)
+            part = tile(f"part{j}", [P, I])
+            part_sum = tile(f"part_sum{j}", [P, 1])
+            if j in (1,):
                 nc.vector.scalar_tensor_tensor(
-                    penalty[:],
-                    sums[:],
-                    -1.0 / GROUP,
-                    caution_rows[:, ks].unsqueeze(1).to_broadcast([P, 4, 16]),
-                    ALU.mult,
-                    ALU.mult,
+                    part[:], part_root[:], 1.0, part_root[:], ALU.mult, ALU.mult, accum_out=part_sum[:]
                 )
-                nc.vector.tensor_tensor(result[:, :, ks], best[:], penalty[:], ALU.add)
+            else:
+                nc.scalar.activation(part[:], part_root[:], ACT.Square, accum_out=part_sum[:])
+            held[j] = part, part_sum
+
+        def weights(j):
+            part, part_sum = held[j]
+            inv_sum = tile(f"inv_sum{j}", [P, 1])
+            nc.vector.reciprocal(inv_sum[:], part_sum[:])
+            w_rows = tile(f"w_rows{j}", [P, I], BF16)
+            nc.vector.scalar_tensor_tensor(w_rows[:], part[:], inv_sum[:], os_rows[:], ALU.mult, ALU.mult)
+            w_turned = bank(f"turn{j % 2}", f"w_turned{j}", [P, 2, P])
+            for u in range(2):
+                nc.tensor.transpose(w_turned[:, u, :], w_rows[:].bitcast(F32)[:, u::2], ident[:])
+            held[j] = w_turned
+
+        def product(j):
+            w_turned = held[j]
+            w_bf = tile(f"w_bf{j}", [P, 4 * P], BF16)
+            (nc.vector.tensor_copy if j in () else nc.scalar.copy)(
+                w_bf[:].bitcast(F32).rearrange("p (q u) -> p q u", u=2), w_turned[:].rearrange("p u q -> p q u")
+            )
+            w_codes = tile(f"w_codes{j}", [P, P], U32)
+            w_scales = tile(f"w_scales{j}", [P, P], U8)
+            nc.vector.quantize_mx(out=w_codes[:].bitcast(FP8X4), scales=w_scales[:], in_=w_bf[:])
+            o_bank = bank(s_tags[j], f"o_bank{j}", [P, 4, P])
+            for b in range(4):
+                cols = slice(b * P, (b + 1) * P)
+                nc.tensor.matmul_mx(
+                    o_bank[:, b, :],
+                    lhsT=v_codes[:, cols].bitcast(FP8X4),
+                    lhsT_scale=v_scales[:, cols],
+                    rhs=w_codes[:].bitcast(FP8X4),
+                    rhs_scale=w_scales[:],
+                    start=True,
+                    stop=True,
+                )
+            held[j] = o_bank
+
+        def read_out(j):
+            o_bank = held[j]
+            groups = o_bank[:].rearrange("p b (k g) -> p b k g", g=GROUP)
+            ks = slice(16 * j, 16 * (j + 1))
+            sums = tile(f"sums{j}", [P, 4, 16])
+            nc.vector.tensor_reduce(sums[:], groups, AX.X, ALU.add)
+            best = tile(f"best{j}", [P, 4, 16])
+            nc.vector.tensor_reduce(best[:], groups, AX.X, ALU.max)
+            penalty = tile(f"penalty{j}", [P, 4, 16])
+            nc.vector.scalar_tensor_tensor(
+                penalty[:],
+                sums[:],
+                -1.0 / GROUP,
+                caution_rows[:, ks].unsqueeze(1).to_broadcast([P, 4, 16]),
+                ALU.mult,
+                ALU.mult,
+            )
+            nc.vector.tensor_tensor(result[:, :, ks], best[:], penalty[:], ALU.add)
+
+        stages = (parts, weights, product, read_out)
+        lags = (0,1,2,3)
+        for step in range(4 + max(lags)):
+            for stage, lag in zip(stages, lags):
+                if 0 <= step - lag < 4:
+                    stage(step - lag)
         nc.sync.dma_start(out.rearrange("(p j) k -> p j k", j=4), result[:])

@@ -19,9 +19,15 @@ ALU = mybir.AluOpType
 AX = mybir.AxisListType
 
 P = 128
-GROUP = Q // K
+TILES = 4
+PACK = 4
 HALF = Q // 2
-TINY = 2.0 ** -60
+GROUP = Q // K
+TILE_GROUPS = P // GROUP
+LAST = TILES - 1
+TINY = 2.0**-60
+CHUNKS = ((0,), (1,), (2, 3))
+TILE_BANKS = ("side0", "side1", "main0", "main2")
 
 
 def tile_attend_saturating_typical_groupbestread_kernel(
@@ -40,6 +46,17 @@ def tile_attend_saturating_typical_groupbestread_kernel(
 
         def add_transposed(dst, src, start, stop):
             nc.tensor.matmul(dst, lhsT=src, rhs=ident[:], is_transpose=True, start=start, stop=stop)
+
+        def product_mx(dst, stationary, stationary_scales, moving, moving_scales):
+            nc.tensor.matmul_mx(
+                dst,
+                lhsT=stationary.bitcast(FP8X4),
+                lhsT_scale=stationary_scales,
+                rhs=moving.bitcast(FP8X4),
+                rhs_scale=moving_scales,
+                start=True,
+                stop=True,
+            )
 
         offsets = tile("offsets", [P, I // 16], U16)
         nc.sync.dma_start(offsets[:], offs)
@@ -62,33 +79,33 @@ def tile_attend_saturating_typical_groupbestread_kernel(
                 key_scale_pool[32 * quad : 32 * quad + 4, :].bitcast(I32),
                 keys_scales[0, 4 * quad : 4 * quad + 4, :].bitcast(I32),
             )
-        q_rows = query.rearrange("(p j) q -> p j q", j=4)
-        q_raw = [tile(f"q_raw{h}", [P, 4, HALF]) for h in range(2)]
+        q_rows = query.rearrange("(p t) q -> p t q", t=PACK)
+        q_raw = [tile(f"q_raw{h}", [P, PACK, HALF]) for h in range(2)]
         key_pool = tile("key_pool", [P, T], I32)
         nc.sync.dma_start(q_raw[0][:], q_rows[:, :, 0:HALF])
         nc.sync.dma_start(key_pool[:], keys_words[0].rearrange("p n t -> p (n t)").bitcast(I32))
         nc.sync.dma_start(q_raw[1][:], q_rows[:, :, HALF:Q])
-        width_cols = tile("width_cols", [P, 4])
+        width_cols = tile("width_cols", [P, TILES])
         nc.sync.dma_start(
             width_cols[:], width.rearrange("(j p) o -> p (j o)", p=P), allow_slow_non_contiguous=True
         )
-        val_rows = vals.rearrange("(p j) t -> j p t", j=4)
-        val_pool = [tile(f"val_pool{b}", [P, T]) for b in range(4)]
-        for b in range(4):
+        val_rows = vals.rearrange("(p b) t -> b p t", b=TILES)
+        val_pool = [tile(f"val_pool{b}", [P, T]) for b in range(TILES)]
+        for b in range(TILES):
             nc.sync.dma_start(val_pool[b][:], val_rows[b])
         os_rows = tile("os_rows", [P, I])
         nc.sync.dma_start(os_rows[:], os_row[0].partition_broadcast(P))
         caution_rows = tile("caution_rows", [P, K])
         nc.sync.dma_start(caution_rows[:], caution[0].partition_broadcast(P))
 
-        cols_of = {}
-        for name, pool, tag in (("half", half_pool, "side0"), ("ceil", ceil_pool, "side1")):
+        listed_cols = {}
+        for name, window, tag in (("half", half_pool, "side0"), ("ceil", ceil_pool, "side1")):
             picked = tile(f"{name}_picked", [P, I])
-            nc.scalar.activation(picked[:], pool[:].indirect(offsets[:]), ACT.Copy)
-            turned = bank(tag, f"{name}_turned", [P, 4, P])
-            for s in range(4):
+            nc.scalar.activation(picked[:], window[:].indirect(offsets[:]), ACT.Copy)
+            turned = bank(tag, f"{name}_turned", [P, TILES, P])
+            for s in range(TILES):
                 nc.tensor.transpose(turned[:, s, :], picked[:, s * P : (s + 1) * P], ident[:])
-            cols_of[name] = turned[:, :, P - 1]
+            listed_cols[name] = turned[:, :, P - 1]
 
         key_scales = tile("key_scales", [P, I], U8)
         nc.vector.tensor_copy(key_scales[:], key_scale_pool[:].indirect(offsets[:]))
@@ -97,7 +114,7 @@ def tile_attend_saturating_typical_groupbestread_kernel(
         sig = [tile(f"sig{g}", [P, 2, 2 * HALF]) for g in range(2)]
         score = {}
         for h in range(2):
-            q_bf = tile(f"q_bf{h}", [P, HALF, 4], BF16)
+            q_bf = tile(f"q_bf{h}", [P, HALF, PACK], BF16)
             nc.vector.tensor_copy(
                 q_bf[:].rearrange("p (c i) t -> p c t i", i=4),
                 q_raw[h][:].rearrange("p t (c i) -> p c t i", i=4),
@@ -110,73 +127,61 @@ def tile_attend_saturating_typical_groupbestread_kernel(
             for g in range(2):
                 if h == 0:
                     nc.vector.tensor_copy(
-                        key_codes[:, g * 256 : (g + 1) * 256],
+                        key_codes[:, 2 * g * P : 2 * (g + 1) * P],
                         key_pool[:].bitcast(U32).indirect(offsets[:, 16 * g : 16 * (g + 1)]),
                     )
                 score[h, g] = bank(f"main{2 * h + g}", f"score{h}{g}", [P, 2, HALF])
                 for r in range(2):
                     cols = slice((2 * g + r) * P, (2 * g + r + 1) * P)
-                    nc.tensor.matmul_mx(
-                        score[h, g][:, r, :],
-                        lhsT=key_codes[:, cols].bitcast(FP8X4),
-                        lhsT_scale=key_scales[:, cols],
-                        rhs=q_codes[:].bitcast(FP8X4),
-                        rhs_scale=q_scales[:],
-                        start=True,
-                        stop=True,
-                    )
+                    product_mx(score[h, g][:, r, :], key_codes[:, cols], key_scales[:, cols], q_codes[:], q_scales[:])
                 nc.scalar.activation(
                     sig[g][:, h, :], score[h, g][:].rearrange("p r q -> p (r q)"), ACT.Sigmoid, scale=-2.0
                 )
 
-        neg_half = tile("neg_half", [P, 4], tag="q_scales1")
-        nc.scalar.activation(neg_half[:], cols_of["half"], ACT.Copy, scale=-1.0)
-        ceil_cols = tile("ceil_cols", [P, 4], tag="q_codes1")
-        ceil_sum = tile("ceil_sum", [P, 1])
-        nc.scalar.activation(ceil_cols[:], cols_of["ceil"], ACT.Identity, accum_out=ceil_sum[:])
-        neg_ch = tile("neg_ch", [P, 4])
+        neg_half = tile("neg_half", [P, TILES], tag="q_scales1")
+        nc.scalar.activation(neg_half[:], listed_cols["half"], ACT.Copy, scale=-1.0)
+        ceil_cols = tile("ceil_cols", [P, TILES], tag="q_codes1")
+        nc.scalar.copy(ceil_cols[:], listed_cols["ceil"])
+        neg_ch = tile("neg_ch", [P, TILES])
         nc.gpsimd.tensor_tensor(neg_ch[:], neg_half[:], ceil_cols[:], ALU.mult)
 
         v_codes = tile("v_codes", [P, E], U32)
         v_scales = tile("v_scales", [P, E], U8)
 
-        v_turned = {}
-
-        def turn_values(b, tag=None):
+        def turn_values(b, turned, tag=None):
             v_picked = tile(f"v_picked{b}", [P, I], BF16, tag=tag)
             nc.vector.tensor_copy(v_picked[:], val_pool[b][:].indirect(offsets[:]))
-            if b < 3:
-                v_turned[b] = bank(f"turn{b % 2}", f"v_turned{b}", [P, 2, 2, P])
             for u in range(2):
-                nc.tensor.transpose(v_turned[min(b, 2)][:, b // 3, u, :], v_picked[:].bitcast(F32)[:, u::2], ident[:])
+                nc.tensor.transpose(turned[:, u, :], v_picked[:].bitcast(F32)[:, u::2], ident[:])
 
-        def quantise_values(first, n, copy, tag=None):
-            v_bf = tile(f"v_bf{first}", [P, n * 4 * P], BF16, tag=tag)
+        def quantise_values(first, count, turned, copy, tag=None):
+            v_bf = tile(f"v_bf{first}", [P, count * PACK * P], BF16, tag=tag)
             copy(
-                v_bf[:].bitcast(F32).rearrange("p (b e u) -> p b e u", b=n, u=2),
-                v_turned[first][:, 0:n].rearrange("p b u e -> p b e u"),
+                v_bf[:].bitcast(F32).rearrange("p (b e u) -> p b e u", b=count, u=2),
+                turned[:, 0:count].rearrange("p b u e -> p b e u"),
             )
-            cols = slice(first * P, (first + n) * P)
+            cols = slice(first * P, (first + count) * P)
             nc.vector.quantize_mx(out=v_codes[:, cols].bitcast(FP8X4), scales=v_scales[:, cols], in_=v_bf[:])
 
-        turn_values(0)
-        quantise_values(0, 1, nc.vector.tensor_copy)
-        turn_values(1)
+        v_turned0 = bank("turn0", "v_turned0", [P, 2, 2, P])
+        turn_values(0, v_turned0[:, 0])
+        v_turned12 = bank("turn1", "v_turned12", [P, 2, 2, P])
+        turn_values(1, v_turned12[:, 0])
 
-        s_tags = ["side0", "side1", "main0", "main2"]
         s_bank = {}
 
         def open_s_bank(j):
-            s_bank[j] = bank(s_tags[j], f"s_bank{j}", [P, 4, P])
-            for s in range(4):
+            s_bank[j] = bank(TILE_BANKS[j], f"s_bank{j}", [P, TILES, P])
+            for s in range(TILES):
                 add_transposed(s_bank[j][:, s, :], ceil_cols[:, s : s + 1].to_broadcast([P, P]), s == 0, False)
 
         open_s_bank(0)
         open_s_bank(1)
+        quantise_values(0, 1, v_turned0, nc.vector.tensor_copy)
 
         neg_fa = {}
         for g in range(2):
-            log_sig = tile(f"log_sig{g}", [P, 2, Q])
+            log_sig = tile(f"log_sig{g}", [P, 2, 2 * HALF])
             nc.scalar.activation(log_sig[:], sig[g][:], ACT.Ln, bias=tiny[:])
             for h in range(2):
                 neg_fa[h, g] = tile(f"neg_fa{h}{g}", [P, 2, HALF])
@@ -189,71 +194,64 @@ def tile_attend_saturating_typical_groupbestread_kernel(
                     ALU.min,
                 )
 
-        quantise_values(1, 1, nc.vector.tensor_copy, "log_sig1")
-        inv_width = tile("inv_width", [P, 4])
+        inv_width = tile("inv_width", [P, TILES])
         nc.vector.reciprocal(inv_width[:], width_cols[:])
 
-        shifts = {}
-        for c, (tiles, sum_tag) in enumerate((((0,), None), ((1,), None), ((2, 3), None))):
-            n = len(tiles)
-            if sum_tag:
-                row_sum = bank(sum_tag, f"row_sum{c}", [P, n, P])
-            for jj, j in enumerate(tiles):
-                if j not in s_bank:
-                    open_s_bank(j)
-                if sum_tag:
-                    add_transposed(row_sum[:, jj, :], ceil_sum[:].to_broadcast([P, P]), jj == 0, False)
-            for s in range(4):
-                root = tile(f"root{c}{s}", [P, n * P])
+        roots = {}
+        for c, chunk in enumerate(CHUNKS):
+            h, first = divmod(chunk[0], 2)
+            for s in range(TILES):
+                roots[c, s] = tile(f"root{c}{s}", [P, len(chunk) * P])
                 nc.scalar.activation(
-                    root[:],
-                    neg_fa[tiles[0] // 2, s // 2][:, s % 2, tiles[0] % 2 * P : (tiles[0] % 2 + n) * P],
+                    roots[c, s][:],
+                    neg_fa[h, s // 2][:, s % 2, first * P : (first + len(chunk)) * P],
                     ACT.Abs_reciprocal_sqrt,
                     bias=neg_half[:, s : s + 1],
                 )
-                drop = tile(f"drop{c}{s}", [P, n * P])
-                nc.vector.scalar_tensor_tensor(drop[:], root[:], neg_ch[:, s : s + 1], root[:], ALU.mult, ALU.mult)
-                for jj in range(n if sum_tag else 0):
-                    add_transposed(row_sum[:, jj, :], drop[:, jj * P : (jj + 1) * P], False, s == 3 and jj == n - 1)
-                for jj, j in enumerate(tiles):
-                    add_transposed(s_bank[j][:, s, :], drop[:, jj * P : (jj + 1) * P], False, s == 3)
-            if sum_tag:
-                total = tile(f"total{c}", [P, n])
-                nc.vector.tensor_reduce(total[:], row_sum[:], AX.X, ALU.add)
-                shift = tile(f"shift{c}", [P, n])
-                nc.vector.scalar_tensor_tensor(
-                    shift[:], total[:], -1.0 / I, inv_width[:, tiles[0] : tiles[0] + n], ALU.mult, ALU.mult
-                )
-                for jj, j in enumerate(tiles):
-                    shifts[j] = shift[:, jj : jj + 1]
-            else:
-                for j in tiles:
-                    total = tile(f"total{j}", [P, 1])
-                    nc.vector.tensor_reduce(total[:], s_bank[j][:].rearrange("p s i -> p (s i)"), AX.X, ALU.add)
-                    shift = tile(f"shift{j}", [P, 1])
-                    nc.vector.scalar_tensor_tensor(shift[:], total[:], -1.0 / I, inv_width[:, j : j + 1], ALU.mult, ALU.mult)
-                    shifts[j] = shift[:]
-        turn_values(2, "total0")
-        turn_values(3, "total1")
-        quantise_values(2, 2, nc.scalar.copy, None)
+        open_s_bank(2)
+        open_s_bank(3)
 
-        result = tile("result", [P, 4, K])
+        result = tile("result", [P, TILES, K])
+        neg_caution = tile("neg_caution", [P, K])
+        nc.gpsimd.tensor_scalar(neg_caution[:], caution_rows[:], -1.0 / GROUP, 0.0, ALU.mult, ALU.add)
+
         held = {}
+        for c, chunk in enumerate(CHUNKS):
+            for s in range(TILES):
+                root = roots[c, s]
+                drop = tile(f"drop{c}{s}", [P, len(chunk) * P])
+                nc.vector.scalar_tensor_tensor(drop[:], root[:], neg_ch[:, s : s + 1], root[:], ALU.mult, ALU.mult)
+                for place, j in enumerate(chunk):
+                    add_transposed(s_bank[j][:, s, :], drop[:, place * P : (place + 1) * P], False, s == LAST)
+            for j in chunk:
+                total = tile(f"total{j}", [P, 1])
+                scaled = tile(f"scaled{j}", [P, I])
+                nc.vector.tensor_scalar(
+                    scaled[:],
+                    s_bank[j][:].rearrange("p s i -> p (s i)"),
+                    inv_width[:, j : j + 1],
+                    None,
+                    ALU.mult,
+                    ALU.add,
+                    accum_out=total[:],
+                )
+                held[j] = scaled, total
+
+        turn_values(2, v_turned12[:, 1], "root13")
+        quantise_values(1, 2, v_turned12, nc.scalar.copy, "root22")
+        v_turned3 = bank("turn0", "v_turned3", [P, 2, 2, P])
+        turn_values(3, v_turned3[:, 0], "root23")
+        quantise_values(3, 1, v_turned3, nc.vector.tensor_copy)
 
         def parts(j):
+            scaled, total = held[j]
             z_sq = tile(f"z_sq{j}", [P, I])
-            nc.scalar.activation(
-                z_sq[:],
-                s_bank[j][:].rearrange("p s i -> p (s i)"),
-                ACT.Square,
-                bias=shifts[j],
-                scale=inv_width[:, j : j + 1],
-            )
+            nc.scalar.activation(z_sq[:], scaled[:], ACT.Square, bias=total[:], scale=-float(I))
             part_root = tile(f"part_root{j}", [P, I])
-            nc.scalar.activation(part_root[:], z_sq[:], ACT.Abs_reciprocal_sqrt, bias=1.0)
+            nc.scalar.activation(part_root[:], z_sq[:], ACT.Abs_reciprocal_sqrt, bias=1.0, scale=1.0 / (I * I))
             part = tile(f"part{j}", [P, I])
             part_sum = tile(f"part_sum{j}", [P, 1])
-            if j in (1,):
+            if j == LAST:
                 nc.vector.scalar_tensor_tensor(
                     part[:], part_root[:], 1.0, part_root[:], ALU.mult, ALU.mult, accum_out=part_sum[:]
                 )
@@ -267,57 +265,41 @@ def tile_attend_saturating_typical_groupbestread_kernel(
             nc.vector.reciprocal(inv_sum[:], part_sum[:])
             w_rows = tile(f"w_rows{j}", [P, I], BF16)
             nc.vector.scalar_tensor_tensor(w_rows[:], part[:], inv_sum[:], os_rows[:], ALU.mult, ALU.mult)
-            w_turned = bank(f"turn{j % 2}", f"w_turned{j}", [P, 2, P])
+            w_turned = bank(("main3", "turn1")[j % 2], f"w_turned{j}", [P, 2, P])
             for u in range(2):
                 nc.tensor.transpose(w_turned[:, u, :], w_rows[:].bitcast(F32)[:, u::2], ident[:])
             held[j] = w_turned
 
         def product(j):
-            w_turned = held[j]
-            w_bf = tile(f"w_bf{j}", [P, 4 * P], BF16)
-            (nc.vector.tensor_copy if j in () else nc.scalar.copy)(
-                w_bf[:].bitcast(F32).rearrange("p (q u) -> p q u", u=2), w_turned[:].rearrange("p u q -> p q u")
+            w_bf = tile(f"w_bf{j}", [P, PACK * P], BF16)
+            nc.scalar.copy(
+                w_bf[:].bitcast(F32).rearrange("p (q u) -> p q u", u=2), held[j][:].rearrange("p u q -> p q u")
             )
             w_codes = tile(f"w_codes{j}", [P, P], U32)
             w_scales = tile(f"w_scales{j}", [P, P], U8)
             nc.vector.quantize_mx(out=w_codes[:].bitcast(FP8X4), scales=w_scales[:], in_=w_bf[:])
-            o_bank = bank(s_tags[j], f"o_bank{j}", [P, 4, P])
-            for b in range(4):
+            o_bank = bank(TILE_BANKS[j], f"o_bank{j}", [P, TILES, P])
+            for b in range(TILES):
                 cols = slice(b * P, (b + 1) * P)
-                nc.tensor.matmul_mx(
-                    o_bank[:, b, :],
-                    lhsT=v_codes[:, cols].bitcast(FP8X4),
-                    lhsT_scale=v_scales[:, cols],
-                    rhs=w_codes[:].bitcast(FP8X4),
-                    rhs_scale=w_scales[:],
-                    start=True,
-                    stop=True,
-                )
+                product_mx(o_bank[:, b, :], v_codes[:, cols], v_scales[:, cols], w_codes[:], w_scales[:])
             held[j] = o_bank
 
         def read_out(j):
-            o_bank = held[j]
-            groups = o_bank[:].rearrange("p b (k g) -> p b k g", g=GROUP)
-            ks = slice(16 * j, 16 * (j + 1))
-            sums = tile(f"sums{j}", [P, 4, 16])
+            groups = held[j][:].rearrange("p b (k g) -> p b k g", g=GROUP)
+            ks = slice(TILE_GROUPS * j, TILE_GROUPS * (j + 1))
+            shape = [P, TILES, TILE_GROUPS]
+            sums = tile(f"sums{j}", shape)
             nc.vector.tensor_reduce(sums[:], groups, AX.X, ALU.add)
-            best = tile(f"best{j}", [P, 4, 16])
+            best = tile(f"best{j}", shape)
             nc.vector.tensor_reduce(best[:], groups, AX.X, ALU.max)
-            penalty = tile(f"penalty{j}", [P, 4, 16])
-            nc.vector.scalar_tensor_tensor(
-                penalty[:],
-                sums[:],
-                -1.0 / GROUP,
-                caution_rows[:, ks].unsqueeze(1).to_broadcast([P, 4, 16]),
-                ALU.mult,
-                ALU.mult,
-            )
-            nc.vector.tensor_tensor(result[:, :, ks], best[:], penalty[:], ALU.add)
+            engine = nc.vector if j == LAST else nc.gpsimd
+            penalty = tile(f"penalty{j}", shape)
+            engine.tensor_tensor(penalty[:], sums[:], neg_caution[:, ks].unsqueeze(1).to_broadcast(shape), ALU.mult)
+            engine.tensor_tensor(result[:, :, ks], best[:], penalty[:], ALU.add)
 
         stages = (parts, weights, product, read_out)
-        lags = (0,1,2,3)
-        for step in range(4 + max(lags)):
-            for stage, lag in zip(stages, lags):
-                if 0 <= step - lag < 4:
+        for step in range(TILES + len(stages) - 1):
+            for lag, stage in enumerate(stages):
+                if 0 <= step - lag < TILES:
                     stage(step - lag)
-        nc.sync.dma_start(out.rearrange("(p j) k -> p j k", j=4), result[:])
+        nc.sync.dma_start(out.rearrange("(p b) k -> p b k", b=TILES), result[:])

@@ -25,6 +25,7 @@ HALF = Q // 2
 GROUP = Q // K
 TILE_GROUPS = P // GROUP
 LAST = TILES - 1
+CAUTION_ROW, WIDTH_ROW, OS_ROW = P - 3, P - 2, P - 1
 TINY = 2.0**-60
 CHUNKS = ((0,), (1,), (2, 3))
 TILE_BANKS = ("side0", "side1", "main0", "main2")
@@ -70,6 +71,8 @@ def tile_attend_saturating_typical_groupbestread_kernel(
         tiny = tile("tiny", [P, 1])
         nc.vector.memset(tiny[:], TINY)
         ident = tile("ident", [P, P])
+        small_rows = tile("small_rows", [P, I])
+        nc.gpsimd.memset(small_rows[:], 0.0)
         make_identity(nc, ident[:])
 
         nc.sync.dma_start(half_pool[P - 1 : P, :], halfp[0:1, :])
@@ -85,18 +88,14 @@ def tile_attend_saturating_typical_groupbestread_kernel(
         nc.sync.dma_start(q_raw[0][:], q_rows[:, :, 0:HALF])
         nc.sync.dma_start(key_pool[:], keys_words[0].rearrange("p n t -> p (n t)").bitcast(I32))
         nc.sync.dma_start(q_raw[1][:], q_rows[:, :, HALF:Q])
-        width_cols = tile("width_cols", [P, TILES])
-        nc.sync.dma_start(
-            width_cols[:], width.rearrange("(j p) o -> p (j o)", p=P), allow_slow_non_contiguous=True
-        )
         val_rows = vals.rearrange("(p b) t -> b p t", b=TILES)
         val_pool = [tile(f"val_pool{b}", [P, T]) for b in range(TILES)]
-        for b in range(TILES):
+        nc.sync.dma_start(val_pool[0][:], val_rows[0])
+        nc.sync.dma_start(small_rows[WIDTH_ROW : WIDTH_ROW + 1, :], width.rearrange("q o -> o q"))
+        nc.sync.dma_start(small_rows[OS_ROW : OS_ROW + 1, :], os_row)
+        nc.sync.dma_start(small_rows[CAUTION_ROW : CAUTION_ROW + 1, 0:K], caution)
+        for b in range(1, TILES):
             nc.sync.dma_start(val_pool[b][:], val_rows[b])
-        os_rows = tile("os_rows", [P, I])
-        nc.sync.dma_start(os_rows[:], os_row[0].partition_broadcast(P))
-        caution_rows = tile("caution_rows", [P, K])
-        nc.sync.dma_start(caution_rows[:], caution[0].partition_broadcast(P))
 
         listed_cols = {}
         for name, window, tag in (("half", half_pool, "side0"), ("ceil", ceil_pool, "side1")):
@@ -144,6 +143,12 @@ def tile_attend_saturating_typical_groupbestread_kernel(
         nc.scalar.copy(ceil_cols[:], listed_cols["ceil"])
         neg_ch = tile("neg_ch", [P, TILES])
         nc.gpsimd.tensor_tensor(neg_ch[:], neg_half[:], ceil_cols[:], ALU.mult)
+
+        small_turned = bank("turn1", "small_turned", [P, TILES, P])
+        for s in range(TILES):
+            nc.tensor.transpose(small_turned[:, s, :], small_rows[:, s * P : (s + 1) * P], ident[:])
+        small_cols = tile("small_cols", [P, TILES, 3])
+        nc.vector.tensor_copy(small_cols[:], small_turned[:, :, CAUTION_ROW:P])
 
         v_codes = tile("v_codes", [P, E], U32)
         v_scales = tile("v_scales", [P, E], U8)
@@ -195,7 +200,7 @@ def tile_attend_saturating_typical_groupbestread_kernel(
                 )
 
         inv_width = tile("inv_width", [P, TILES])
-        nc.vector.reciprocal(inv_width[:], width_cols[:])
+        nc.vector.reciprocal(inv_width[:], small_cols[:, :, 1])
 
         roots = {}
         for c, chunk in enumerate(CHUNKS):
@@ -212,8 +217,13 @@ def tile_attend_saturating_typical_groupbestread_kernel(
         open_s_bank(3)
 
         result = tile("result", [P, TILES, K])
+        os_rows = bank("main1", "os_rows", [P, TILES, P])
+        for s in range(TILES):
+            nc.tensor.transpose(os_rows[:, s, :], small_cols[:, s, 2:3].to_broadcast([P, P]), ident[:])
+        caution_rows = bank("main3", "caution_rows", [P, P])
+        nc.tensor.transpose(caution_rows[:], small_cols[:, 0, 0:1].to_broadcast([P, P]), ident[:])
         neg_caution = tile("neg_caution", [P, K])
-        nc.gpsimd.tensor_scalar(neg_caution[:], caution_rows[:], -1.0 / GROUP, 0.0, ALU.mult, ALU.add)
+        nc.scalar.activation(neg_caution[:], caution_rows[:, 0:K], ACT.Copy, scale=-1.0 / GROUP)
 
         held = {}
         for c, chunk in enumerate(CHUNKS):
@@ -251,12 +261,7 @@ def tile_attend_saturating_typical_groupbestread_kernel(
             nc.scalar.activation(part_root[:], z_sq[:], ACT.Abs_reciprocal_sqrt, bias=1.0, scale=1.0 / (I * I))
             part = tile(f"part{j}", [P, I])
             part_sum = tile(f"part_sum{j}", [P, 1])
-            if j == LAST:
-                nc.vector.scalar_tensor_tensor(
-                    part[:], part_root[:], 1.0, part_root[:], ALU.mult, ALU.mult, accum_out=part_sum[:]
-                )
-            else:
-                nc.scalar.activation(part[:], part_root[:], ACT.Square, accum_out=part_sum[:])
+            nc.scalar.activation(part[:], part_root[:], ACT.Square, accum_out=part_sum[:])
             held[j] = part, part_sum
 
         def weights(j):
@@ -264,7 +269,9 @@ def tile_attend_saturating_typical_groupbestread_kernel(
             inv_sum = tile(f"inv_sum{j}", [P, 1])
             nc.vector.reciprocal(inv_sum[:], part_sum[:])
             w_rows = tile(f"w_rows{j}", [P, I], BF16)
-            nc.vector.scalar_tensor_tensor(w_rows[:], part[:], inv_sum[:], os_rows[:], ALU.mult, ALU.mult)
+            nc.vector.scalar_tensor_tensor(
+                w_rows[:], part[:], inv_sum[:], os_rows[:].rearrange("p s i -> p (s i)"), ALU.mult, ALU.mult
+            )
             w_turned = bank(("main3", "turn1")[j % 2], f"w_turned{j}", [P, 2, P])
             for u in range(2):
                 nc.tensor.transpose(w_turned[:, u, :], w_rows[:].bitcast(F32)[:, u::2], ident[:])

from contextlib import ExitStack

import concourse.mybir as mybir
from concourse.masks import make_identity

D, T, I, Q, E, K = 512, 2048, 512, 512, 512, 64
FLOPS = 2 * Q * I * D + 2 * E * Q * I
BYTES = 4 * (D * Q + 128 * T + E * T + 2 * T + Q + I + K + E * K) + 16 * T + 2 * 128 * 32

F32 = mybir.dt.float32
BF16 = mybir.dt.bfloat16
I32 = mybir.dt.int32
U32 = mybir.dt.uint32
U16 = mybir.dt.uint16
U8 = mybir.dt.uint8
FP8X4 = mybir.dt.float8_e4m3fn_x4
ACT = mybir.ActivationFunctionType
ALU = mybir.AluOpType
AX = mybir.AxisListType

P = 128
TILES = 4
PACK = 4
HALF = Q // 2
GROUP = Q // K
TILE_GROUPS = P // GROUP
LAST = TILES - 1
CAUTION_ROW, WIDTH_ROW, OS_ROW = P - 3, P - 2, P - 1
TINY = 2.0**-60
CHUNKS = ((0,), (1,), (2, 3))
TILE_BANKS = ("side0", "side1", "main0", "main2")


def tile_attend_saturating_typical_groupbestread_kernel(
    tc, query, keys_words, keys_scales, ceil_t, halfp, width, os_row, vals, caution, offs, out
):
    nc = tc.nc
    with ExitStack() as ctx:
        sb = ctx.enter_context(tc.tile_pool(name="sb", bufs=1))
        ps = ctx.enter_context(tc.psum_pool(name="ps", bufs=1))

        def tile(name, shape, dtype=F32, tag=None):
            return sb.tile(shape, dtype, name=name, tag=tag or name, align_bytes=64)

        def bank(tag, name, shape):
            return ps.tile(shape, F32, name=name, tag=tag)

        def add_transposed(dst, src, start, stop):
            nc.tensor.matmul(dst, lhsT=src, rhs=ident[:], is_transpose=True, start=start, stop=stop)

        def product_mx(dst, stationary, stationary_scales, moving, moving_scales):
            nc.tensor.matmul_mx(
                dst,
                lhsT=stationary.bitcast(FP8X4),
                lhsT_scale=stationary_scales,
                rhs=moving.bitcast(FP8X4),
                rhs_scale=moving_scales,
                start=True,
                stop=True,
            )

        offsets = tile("offsets", [P, I // 16], U16)
        nc.sync.dma_start(offsets[:], offs)

        key_scale_pool = tile("key_scale_pool", [P, T], U8)
        nc.gpsimd.memset(key_scale_pool[:].bitcast(I32), 0)
        half_pool = tile("half_pool", [P, T])
        ceil_pool = tile("ceil_pool", [P, T])
        nc.vector.memset(half_pool[0 : P - 1, :], 0.0)
        nc.vector.memset(ceil_pool[0 : P - 1, :], 0.0)
        tiny = tile("tiny", [P, 1])
        nc.vector.memset(tiny[:], TINY)
        ident = tile("ident", [P, P])
        small_rows = tile("small_rows", [P, I])
        nc.gpsimd.memset(small_rows[:], 0.0)
        make_identity(nc, ident[:])

        nc.sync.dma_start(half_pool[P - 1 : P, :], halfp[0:1, :])
        nc.sync.dma_start(ceil_pool[P - 1 : P, :], ceil_t[0:1, :])
        for quad in range(4):
            nc.sync.dma_start(
                key_scale_pool[32 * quad : 32 * quad + 4, :].bitcast(I32),
                keys_scales[0, 4 * quad : 4 * quad + 4, :].bitcast(I32),
            )
        q_rows = query.rearrange("(p t) q -> p t q", t=PACK)
        q_raw = [tile(f"q_raw{h}", [P, PACK, HALF]) for h in range(2)]
        key_pool = tile("key_pool", [P, T], I32)
        nc.sync.dma_start(q_raw[0][:], q_rows[:, :, 0:HALF])
        nc.sync.dma_start(key_pool[:], keys_words[0].rearrange("p n t -> p (n t)").bitcast(I32))
        nc.sync.dma_start(q_raw[1][:], q_rows[:, :, HALF:Q])
        val_rows = vals.rearrange("(p b) t -> b p t", b=TILES)
        val_pool = [tile(f"val_pool{b}", [P, T]) for b in range(TILES)]
        nc.sync.dma_start(val_pool[0][:], val_rows[0])
        nc.sync.dma_start(small_rows[WIDTH_ROW : WIDTH_ROW + 1, :], width.rearrange("q o -> o q"))
        nc.sync.dma_start(small_rows[OS_ROW : OS_ROW + 1, :], os_row)
        nc.sync.dma_start(small_rows[CAUTION_ROW : CAUTION_ROW + 1, 0:K], caution)
        for b in range(1, TILES):
            nc.sync.dma_start(val_pool[b][:], val_rows[b])

        listed_cols = {}
        for name, window, tag in (("half", half_pool, "side0"), ("ceil", ceil_pool, "side1")):
            picked = tile(f"{name}_picked", [P, I])
            nc.scalar.activation(picked[:], window[:].indirect(offsets[:]), ACT.Copy)
            turned = bank(tag, f"{name}_turned", [P, TILES, P])
            for s in range(TILES):
                nc.tensor.transpose(turned[:, s, :], picked[:, s * P : (s + 1) * P], ident[:])
            listed_cols[name] = turned[:, :, P - 1]

        key_scales = tile("key_scales", [P, I], U8)
        nc.vector.tensor_copy(key_scales[:], key_scale_pool[:].indirect(offsets[:]))

        key_codes = tile("key_codes", [P, I], U32)
        sig = [tile(f"sig{g}", [P, 2, 2 * HALF]) for g in range(2)]
        score = {}
        for h in range(2):
            q_bf = tile(f"q_bf{h}", [P, HALF, PACK], BF16)
            nc.vector.tensor_copy(
                q_bf[:].rearrange("p (c i) t -> p c t i", i=4),
                q_raw[h][:].rearrange("p t (c i) -> p c t i", i=4),
            )
            q_codes = tile(f"q_codes{h}", [P, HALF], U32)
            q_scales = tile(f"q_scales{h}", [P, HALF], U8)
            nc.vector.quantize_mx(
                out=q_codes[:].bitcast(FP8X4), scales=q_scales[:], in_=q_bf[:].rearrange("p c t -> p (c t)")
            )
            for g in range(2):
                if h == 0:
                    nc.vector.tensor_copy(
                        key_codes[:, 2 * g * P : 2 * (g + 1) * P],
                        key_pool[:].bitcast(U32).indirect(offsets[:, 16 * g : 16 * (g + 1)]),
                    )
                score[h, g] = bank(f"main{2 * h + g}", f"score{h}{g}", [P, 2, HALF])
                for r in range(2):
                    cols = slice((2 * g + r) * P, (2 * g + r + 1) * P)
                    product_mx(score[h, g][:, r, :], key_codes[:, cols], key_scales[:, cols], q_codes[:], q_scales[:])
                nc.scalar.activation(
                    sig[g][:, h, :], score[h, g][:].rearrange("p r q -> p (r q)"), ACT.Sigmoid, scale=-2.0
                )

        neg_half = tile("neg_half", [P, TILES], tag="q_scales1")
        nc.scalar.activation(neg_half[:], listed_cols["half"], ACT.Copy, scale=-1.0)
        ceil_cols = tile("ceil_cols", [P, TILES], tag="q_codes1")
        nc.scalar.copy(ceil_cols[:], listed_cols["ceil"])
        neg_ch = tile("neg_ch", [P, TILES])
        nc.gpsimd.tensor_tensor(neg_ch[:], neg_half[:], ceil_cols[:], ALU.mult)

        small_turned = bank("turn1", "small_turned", [P, TILES, P])
        for s in range(TILES):
            nc.tensor.transpose(small_turned[:, s, :], small_rows[:, s * P : (s + 1) * P], ident[:])
        small_cols = tile("small_cols", [P, TILES, 3])
        nc.vector.tensor_copy(small_cols[:], small_turned[:, :, CAUTION_ROW:P])

        v_codes = tile("v_codes", [P, E], U32)
        v_scales = tile("v_scales", [P, E], U8)

        def turn_values(b, turned, tag=None):
            v_picked = tile(f"v_picked{b}", [P, I], BF16, tag=tag)
            nc.vector.tensor_copy(v_picked[:], val_pool[b][:].indirect(offsets[:]))
            for u in range(2):
                nc.tensor.transpose(turned[:, u, :], v_picked[:].bitcast(F32)[:, u::2], ident[:])

        def quantise_values(first, count, turned, copy, tag=None):
            v_bf = tile(f"v_bf{first}", [P, count * PACK * P], BF16, tag=tag)
            copy(
                v_bf[:].bitcast(F32).rearrange("p (b e u) -> p b e u", b=count, u=2),
                turned[:, 0:count].rearrange("p b u e -> p b e u"),
            )
            cols = slice(first * P, (first + count) * P)
            nc.vector.quantize_mx(out=v_codes[:, cols].bitcast(FP8X4), scales=v_scales[:, cols], in_=v_bf[:])

        v_turned0 = bank("turn0", "v_turned0", [P, 2, 2, P])
        turn_values(0, v_turned0[:, 0])
        v_turned12 = bank("turn1", "v_turned12", [P, 2, 2, P])
        turn_values(1, v_turned12[:, 0])

        s_bank = {}

        def open_s_bank(j):
            s_bank[j] = bank(TILE_BANKS[j], f"s_bank{j}", [P, TILES, P])
            for s in range(TILES):
                add_transposed(s_bank[j][:, s, :], ceil_cols[:, s : s + 1].to_broadcast([P, P]), s == 0, False)

        open_s_bank(0)
        open_s_bank(1)
        quantise_values(0, 1, v_turned0, nc.vector.tensor_copy)

        neg_fa = {}
        for g in range(2):
            log_sig = tile(f"log_sig{g}", [P, 2, 2 * HALF])
            nc.scalar.activation(log_sig[:], sig[g][:], ACT.Ln, bias=tiny[:])
            for h in range(2):
                neg_fa[h, g] = tile(f"neg_fa{h}{g}", [P, 2, HALF])
                nc.vector.scalar_tensor_tensor(
                    neg_fa[h, g][:].rearrange("p r q -> p (r q)"),
                    score[h, g][:].rearrange("p r q -> p (r q)"),
                    -2.0,
                    log_sig[:, h, :],
                    ALU.mult,
                    ALU.min,
                )

        inv_width = tile("inv_width", [P, TILES])
        nc.vector.reciprocal(inv_width[:], small_cols[:, :, 1])

        roots = {}
        for c, chunk in enumerate(CHUNKS):
            h, first = divmod(chunk[0], 2)
            for s in range(TILES):
                roots[c, s] = tile(f"root{c}{s}", [P, len(chunk) * P])
                nc.scalar.activation(
                    roots[c, s][:],
                    neg_fa[h, s // 2][:, s % 2, first * P : (first + len(chunk)) * P],
                    ACT.Abs_reciprocal_sqrt,
                    bias=neg_half[:, s : s + 1],
                )
        open_s_bank(2)
        open_s_bank(3)

        result = tile("result", [P, TILES, K])
        os_rows = bank("main1", "os_rows", [P, TILES, P])
        for s in range(TILES):
            nc.tensor.transpose(os_rows[:, s, :], small_cols[:, s, 2:3].to_broadcast([P, P]), ident[:])
        caution_rows = bank("main3", "caution_rows", [P, P])
        nc.tensor.transpose(caution_rows[:], small_cols[:, 0, 0:1].to_broadcast([P, P]), ident[:])
        neg_caution = tile("neg_caution", [P, K])
        nc.scalar.activation(neg_caution[:], caution_rows[:, 0:K], ACT.Copy, scale=-1.0 / GROUP)

        held = {}
        for c, chunk in enumerate(CHUNKS):
            for s in range(TILES):
                root = roots[c, s]
                drop = tile(f"drop{c}{s}", [P, len(chunk) * P])
                nc.vector.scalar_tensor_tensor(drop[:], root[:], neg_ch[:, s : s + 1], root[:], ALU.mult, ALU.mult)
                for place, j in enumerate(chunk):
                    add_transposed(s_bank[j][:, s, :], drop[:, place * P : (place + 1) * P], False, s == LAST)
            for j in chunk:
                total = tile(f"total{j}", [P, 1])
                scaled = tile(f"scaled{j}", [P, I])
                nc.vector.tensor_scalar(
                    scaled[:],
                    s_bank[j][:].rearrange("p s i -> p (s i)"),
                    inv_width[:, j : j + 1],
                    None,
                    ALU.mult,
                    ALU.add,
                    accum_out=total[:],
                )
                held[j] = scaled, total

        turn_values(2, v_turned12[:, 1], "root13")
        quantise_values(1, 2, v_turned12, nc.scalar.copy, "root22")
        v_turned3 = bank("turn0", "v_turned3", [P, 2, 2, P])
        turn_values(3, v_turned3[:, 0], "root23")
        quantise_values(3, 1, v_turned3, nc.vector.tensor_copy)

        def parts(j):
            scaled, total = held[j]
            z_sq = tile(f"z_sq{j}", [P, I])
            nc.scalar.activation(z_sq[:], scaled[:], ACT.Square, bias=total[:], scale=-float(I))
            part_root = tile(f"part_root{j}", [P, I])
            nc.scalar.activation(part_root[:], z_sq[:], ACT.Abs_reciprocal_sqrt, bias=1.0, scale=1.0 / (I * I))
            part = tile(f"part{j}", [P, I])
            part_sum = tile(f"part_sum{j}", [P, 1])
            nc.scalar.activation(part[:], part_root[:], ACT.Square, accum_out=part_sum[:])
            held[j] = part, part_sum

        def weights(j):
            part, part_sum = held[j]
            inv_sum = tile(f"inv_sum{j}", [P, 1])
            nc.vector.reciprocal(inv_sum[:], part_sum[:])
            w_rows = tile(f"w_rows{j}", [P, I], BF16)
            nc.vector.scalar_tensor_tensor(
                w_rows[:], part[:], inv_sum[:], os_rows[:].rearrange("p s i -> p (s i)"), ALU.mult, ALU.mult
            )
            w_turned = bank(("main3", "turn1")[j % 2], f"w_turned{j}", [P, 2, P])
            for u in range(2):
                nc.tensor.transpose(w_turned[:, u, :], w_rows[:].bitcast(F32)[:, u::2], ident[:])
            held[j] = w_turned

        def product(j):
            w_bf = tile(f"w_bf{j}", [P, PACK * P], BF16)
            nc.scalar.copy(
                w_bf[:].bitcast(F32).rearrange("p (q u) -> p q u", u=2), held[j][:].rearrange("p u q -> p q u")
            )
            w_codes = tile(f"w_codes{j}", [P, P], U32)
            w_scales = tile(f"w_scales{j}", [P, P], U8)
            nc.vector.quantize_mx(out=w_codes[:].bitcast(FP8X4), scales=w_scales[:], in_=w_bf[:])
            o_bank = bank(TILE_BANKS[j], f"o_bank{j}", [P, TILES, P])
            for b in range(TILES):
                cols = slice(b * P, (b + 1) * P)
                product_mx(o_bank[:, b, :], v_codes[:, cols], v_scales[:, cols], w_codes[:], w_scales[:])
            held[j] = o_bank

        def read_out(j):
            groups = held[j][:].rearrange("p b (k g) -> p b k g", g=GROUP)
            ks = slice(TILE_GROUPS * j, TILE_GROUPS * (j + 1))
            shape = [P, TILES, TILE_GROUPS]
            sums = tile(f"sums{j}", shape)
            nc.vector.tensor_reduce(sums[:], groups, AX.X, ALU.add)
            best = tile(f"best{j}", shape)
            nc.vector.tensor_reduce(best[:], groups, AX.X, ALU.max)
            engine = nc.vector if j == LAST else nc.gpsimd
            penalty = tile(f"penalty{j}", shape)
            engine.tensor_tensor(penalty[:], sums[:], neg_caution[:, ks].unsqueeze(1).to_broadcast(shape), ALU.mult)
            engine.tensor_tensor(result[:, :, ks], best[:], penalty[:], ALU.add)

        stages = (parts, weights, product, read_out)
        for step in range(TILES + len(stages) - 1):
            for lag, stage in enumerate(stages):
                if 0 <= step - lag < TILES:
                    stage(step - lag)
        nc.sync.dma_start(out.rearrange("(p b) k -> p b k", b=TILES), result[:])
